import numpy as np, ml_dtypes
CORES = [66,70,74,78,82,86,90,94,98,102,106,110,114,118,122,126]
N = 16
R, TK = 16, 256
def setup_inputs(rng):
    u = (rng.standard_normal((N, 128, R), dtype=np.float32) / 11).astype(ml_dtypes.bfloat16)
    return {"x": rng.standard_normal((N, 128, TK), dtype=np.float32).astype(ml_dtypes.bfloat16), "u": u, "ut": u.transpose(0, 2, 1).copy(), "vt": rng.standard_normal((N, R, 128), dtype=np.float32).astype(ml_dtypes.bfloat16)}
def setup_inputs_big(rng):
    d = setup_inputs(rng)
    for k in ("x", "u", "ut", "vt"): d[k] = (d[k].astype(np.float32) * 1024.0).astype(d[k].dtype)
    return d
def setup_inputs_small(rng):
    d = setup_inputs(rng)
    for k in ("x", "u", "ut", "vt"): d[k] = (d[k].astype(np.float32) * (1 / 1024.0)).astype(d[k].dtype)
    return d
def setup_inputs_apart(rng):
    d = setup_inputs(rng)
    f = (10.0 ** rng.permutation(np.linspace(-1.5, 1.5, N))).astype(np.float32).reshape(N, 1, 1)
    for k in ("x", "u", "ut", "vt"): d[k] = (d[k].astype(np.float32) * f).astype(d[k].dtype)
    return d
def reference(x, u, ut, vt):
    X, U, VT = x.astype(np.float64), u.astype(np.float64), vt.astype(np.float64)
    y = np.stack([sum(VT[j].T @ (U[j].T @ X[r]) for j in range(N)) for r in range(N)])
    return {"y": y.astype(ml_dtypes.bfloat16)}

@@ -1,0 +1,71 @@
+from concourse.bass import DstId, RemoteDMATransfer
+
+N = 16
+HALF = 64
+
+SCRATCH = {
+    "gath": ("dram", [N, 128, 32], "bfloat16"),
+    "a": ("sbuf", [128, 256], "bfloat16"),
+    "b": ("sbuf", [128, 256], "bfloat16"),
+    "xs": ("sbuf", [128, 256], "bfloat16"),
+    "mt": ("sbuf", [128, 128], "bfloat16"),
+    "ys": ("sbuf", [128, 256], "bfloat16"),
+    "pm": ("psum", [128, 512], "float32"),
+    "py": ("psum", [128, 512], "float32"),
+}
+SEMAPHORES = ["ld", "xl", "arr", "sent", "ab", "m1", "c1", "m2", "c2", "st"]
+
+
+def _bits(mask):
+    return [e for e in range(mask.bit_length()) if (mask >> e) & 1]
+
+
+def rank_program(g, core, T, topo):
+    rank = T.rank_of(core)
+    if rank is None:
+        return
+    S = T.sem
+    n = len(T.cores)
+    mine = T.gath[rank]
+
+    g.sync.dma_start(T.gath[rank, 0:HALF, :], T.ut[:]).then_inc(S.ld, 16)
+    g.scalar.dma_start(T.gath[rank, HALF:128, :], T.vt[:]).then_inc(S.ld, 16)
+    g.sync.dma_start(T.xs[:], T.x[:]).then_inc(S.xl, 16)
+
+    peers = [T.cores[(rank + k) % n] for k in range(1, n)]
+    mask = topo.mask(core, peers[0])
+    for p in peers:
+        assert topo.may_write(core, p)
+        mask &= topo.mask(core, p)
+    ne = len(_bits(mask))
+    ids = []
+    for p in peers:
+        rid, pid, _ = topo.addr(p)
+        ids.append(DstId(rid=rid, pnc=pid))
+    g.wait_ge(S.ld, 32)
+    g.remote_dma_fused(
+        [RemoteDMATransfer(dst_ids=ids, dma_engine_mask=mask, remote_sem=S.arr,
+                           srcs=[mine], dsts=[mine for _ in peers], alu_op=0)],
+        local_sem=S.sent)
+
+    g.sync.wait_ge(S.ld, 32)
+    g.sync.wait_ge(S.arr, ne * len(peers))
+    g.sync.dma_start(T.a[:], T.gath[:, 0:HALF, :]).then_inc(S.ab, 16)
+    g.scalar.wait_ge(S.ld, 32)
+    g.scalar.wait_ge(S.arr, ne * len(peers))
+    g.scalar.dma_start(T.b[:], T.gath[:, HALF:128, :]).then_inc(S.ab, 16)
+
+    g.tensor.wait_ge(S.ab, 32)
+    g.tensor.matmul(T.pm[:, 0:128], T.a[:, 0:128], T.b[:, 0:128], start=True, stop=False)
+    g.tensor.matmul(T.pm[:, 0:128], T.a[:, 128:256], T.b[:, 128:256], start=False, stop=True).then_inc(S.m1, 1)
+    g.vector.wait_ge(S.m1, 1)
+    g.vector.tensor_copy(T.mt[:], T.pm[:, 0:128]).then_inc(S.c1, 1)
+    g.tensor.wait_ge(S.xl, 16)
+    g.tensor.wait_ge(S.c1, 1)
+    g.tensor.matmul(T.py[:, 0:256], T.mt[:], T.xs[:], start=True, stop=True).then_inc(S.m2, 1)
+    g.vector.wait_ge(S.m2, 1)
+    g.vector.tensor_copy(T.ys[:], T.py[:, 0:256]).then_inc(S.c2, 1)
+    g.sync.wait_ge(S.c2, 1)
+    g.sync.dma_start(T.y[:], T.ys[:]).then_inc(S.st, 16)
+    g.sync.wait_ge(S.st, 16)
+    g.wait_ge(S.sent, ne)

@@ -2,6 +2,7 @@ from concourse.bass import DstId, RemoteDMATransfer
 
 N = 16
 HALF = 64
+GROUPS = (7, 6, 2)
 
 SCRATCH = {
     "gath": ("dram", [N, 128, 32], "bfloat16"),
@@ -11,9 +12,10 @@ SCRATCH = {
     "mt": ("sbuf", [128, 128], "bfloat16"),
     "ys": ("sbuf", [128, 256], "bfloat16"),
     "pm": ("psum", [128, 512], "float32"),
-    "py": ("psum", [128, 512], "float32"),
+    "py0": ("psum", [128, 512], "float32"),
+    "py1": ("psum", [128, 512], "float32"),
 }
-SEMAPHORES = ["ld", "xl", "arr", "sent", "ab", "m1", "c1", "m2", "c2", "st"]
+SEMAPHORES = ["ld", "xl", "arr0", "arr1", "arr2", "sent", "ab", "m1", "c1", "m20", "m21", "c20", "c21", "st"]
 
 
 def _bits(mask):
@@ -26,46 +28,56 @@ def rank_program(g, core, T, topo):
         return
     S = T.sem
     n = len(T.cores)
-    mine = T.gath[rank]
 
-    g.sync.dma_start(T.gath[rank, 0:HALF, :], T.ut[:]).then_inc(S.ld, 16)
-    g.scalar.dma_start(T.gath[rank, HALF:128, :], T.vt[:]).then_inc(S.ld, 16)
+    g.sync.dma_start(T.gath[0, 0:HALF, :], T.ut[:]).then_inc(S.ld, 16)
+    g.scalar.dma_start(T.gath[0, HALF:128, :], T.vt[:]).then_inc(S.ld, 16)
     g.sync.dma_start(T.xs[:], T.x[:]).then_inc(S.xl, 16)
 
-    peers = [T.cores[(rank + k) % n] for k in range(1, n)]
-    mask = topo.mask(core, peers[0])
-    for p in peers:
+    peer = {k: T.cores[(rank + k) % n] for k in range(1, n)}
+    mask = topo.mask(core, peer[1])
+    for p in peer.values():
         assert topo.may_write(core, p)
         mask &= topo.mask(core, p)
     ne = len(_bits(mask))
-    ids = []
-    for p in peers:
-        rid, pid, _ = topo.addr(p)
-        ids.append(DstId(rid=rid, pnc=pid))
+
     g.wait_ge(S.ld, 32)
-    g.remote_dma_fused(
-        [RemoteDMATransfer(dst_ids=ids, dma_engine_mask=mask, remote_sem=S.arr,
-                           srcs=[mine], dsts=[mine for _ in peers], alu_op=0)],
-        local_sem=S.sent)
+    first = 1
+    spans = []
+    for i, cnt in enumerate(GROUPS):
+        dists = range(first, first + cnt)
+        ids = []
+        for k in dists:
+            rid, pid, _ = topo.addr(peer[k])
+            ids.append(DstId(rid=rid, pnc=pid))
+        g.remote_dma_fused(
+            [RemoteDMATransfer(dst_ids=ids, dma_engine_mask=mask, remote_sem=S["arr%d" % i],
+                               srcs=[T.gath[0]], dsts=[T.gath[k] for k in dists], alu_op=0)],
+            local_sem=S.sent)
+        spans.append((first if i else 0, first + cnt, S["arr%d" % i], cnt))
+        first += cnt
 
-    g.sync.wait_ge(S.ld, 32)
-    g.sync.wait_ge(S.arr, ne * len(peers))
-    g.sync.dma_start(T.a[:], T.gath[:, 0:HALF, :]).then_inc(S.ab, 16)
-    g.scalar.wait_ge(S.ld, 32)
-    g.scalar.wait_ge(S.arr, ne * len(peers))
-    g.scalar.dma_start(T.b[:], T.gath[:, HALF:128, :]).then_inc(S.ab, 16)
+    for q, dst, lo, hi in ((g.sync, T.a, 0, HALF), (g.scalar, T.b, HALF, 128)):
+        q.wait_ge(S.ld, 32)
+        for s0, s1, sem, cnt in spans:
+            q.wait_ge(sem, ne * cnt)
+            q.dma_start(dst[8 * s0:8 * s1, :], T.gath[s0:s1, lo:hi, :]).then_inc(S.ab, 16)
 
-    g.tensor.wait_ge(S.ab, 32)
+    g.tensor.wait_ge(S.ab, 32 * len(spans))
     g.tensor.matmul(T.pm[:, 0:128], T.a[:, 0:128], T.b[:, 0:128], start=True, stop=False)
     g.tensor.matmul(T.pm[:, 0:128], T.a[:, 128:256], T.b[:, 128:256], start=False, stop=True).then_inc(S.m1, 1)
     g.vector.wait_ge(S.m1, 1)
     g.vector.tensor_copy(T.mt[:], T.pm[:, 0:128]).then_inc(S.c1, 1)
     g.tensor.wait_ge(S.xl, 16)
     g.tensor.wait_ge(S.c1, 1)
-    g.tensor.matmul(T.py[:, 0:256], T.mt[:], T.xs[:], start=True, stop=True).then_inc(S.m2, 1)
-    g.vector.wait_ge(S.m2, 1)
-    g.vector.tensor_copy(T.ys[:], T.py[:, 0:256]).then_inc(S.c2, 1)
-    g.sync.wait_ge(S.c2, 1)
-    g.sync.dma_start(T.y[:], T.ys[:]).then_inc(S.st, 16)
-    g.sync.wait_ge(S.st, 16)
-    g.wait_ge(S.sent, ne)
+    g.tensor.matmul(T.py0[:, 0:128], T.mt[:], T.xs[:, 0:128], start=True, stop=True).then_inc(S.m20, 1)
+    g.tensor.matmul(T.py1[:, 0:128], T.mt[:], T.xs[:, 128:256], start=True, stop=True).then_inc(S.m21, 1)
+    g.vector.wait_ge(S.m20, 1)
+    g.vector.tensor_copy(T.ys[:, 0:128], T.py0[:, 0:128]).then_inc(S.c20, 1)
+    g.vector.wait_ge(S.m21, 1)
+    g.vector.tensor_copy(T.ys[:, 128:256], T.py1[:, 0:128]).then_inc(S.c21, 1)
+    g.scalar.wait_ge(S.c20, 1)
+    g.scalar.dma_start(T.y[:, 0:128], T.ys[:, 0:128]).then_inc(S.st, 16)
+    g.sync.wait_ge(S.c21, 1)
+    g.sync.dma_start(T.y[:, 128:256], T.ys[:, 128:256]).then_inc(S.st, 16)
+    g.sync.wait_ge(S.st, 32)
+    g.wait_ge(S.sent, ne * len(GROUPS))

@@ -1,25 +1,44 @@
 from concourse.bass import DstId, RemoteDMATransfer
+from concourse.mybir import dt, AluOpType, AxisListType, ActivationFunctionType
 
 N = 16
 HALF = 64
 GROUPS = (7, 6, 2)
+T0 = 8
 
 SCRATCH = {
     "gath": ("dram", [N, 128, 32], "bfloat16"),
-    "a": ("sbuf", [128, 256], "bfloat16"),
-    "b": ("sbuf", [128, 256], "bfloat16"),
+    "a0": ("sbuf", [128, 256], "bfloat16"),
+    "b0": ("sbuf", [128, 256], "bfloat16"),
+    "a1": ("sbuf", [128, 128], "bfloat16"),
+    "b1": ("sbuf", [128, 128], "bfloat16"),
     "xs": ("sbuf", [128, 256], "bfloat16"),
     "mt": ("sbuf", [128, 128], "bfloat16"),
     "ys": ("sbuf", [128, 256], "bfloat16"),
-    "pm": ("psum", [128, 512], "float32"),
+    "pma": ("psum", [128, 512], "float32"),
+    "pmb": ("psum", [128, 512], "float32"),
     "py0": ("psum", [128, 512], "float32"),
     "py1": ("psum", [128, 512], "float32"),
+    "py2": ("psum", [128, 512], "float32"),
+    "py3": ("psum", [128, 512], "float32"),
 }
-SEMAPHORES = ["ld", "xl", "arr0", "arr1", "arr2", "sent", "ab", "m1", "c1", "m20", "m21", "c20", "c21", "st"]
+SEMAPHORES = ["ld", "xl", "arr0", "arr1", "arr2", "sent", "ab0", "ab1", "ma", "mb", "c1",
+              "y0", "y1", "y2", "y3", "cy01", "cy23", "st"]
 
 
 def _bits(mask):
     return [e for e in range(mask.bit_length()) if (mask >> e) & 1]
+
+
+def _way(topo, a, b):
+    ca, cb = topo.chip(a), topo.chip(b)
+    if ca == cb:
+        return 0
+    if topo.mates(ca, cb):
+        return 1
+    if topo.same_plane(ca, cb):
+        return 2
+    return 3
 
 
 def rank_program(g, core, T, topo):
@@ -28,21 +47,27 @@ def rank_program(g, core, T, topo):
         return
     S = T.sem
     n = len(T.cores)
+    copy = ActivationFunctionType.Copy
 
     g.sync.dma_start(T.gath[0, 0:HALF, :], T.ut[:]).then_inc(S.ld, 16)
     g.scalar.dma_start(T.gath[0, HALF:128, :], T.vt[:]).then_inc(S.ld, 16)
     g.sync.dma_start(T.xs[:], T.x[:]).then_inc(S.xl, 16)
 
-    peer = {k: T.cores[(rank + k) % n] for k in range(1, n)}
+    assert n & (n - 1) == 0
+    order = sorted(range(1, n),
+                   key=lambda k: (-max(_way(topo, T.cores[r], T.cores[r ^ k]) for r in range(n)), k))
+    peer = {i + 1: T.cores[rank ^ k] for i, k in enumerate(order)}
     mask = topo.mask(core, peer[1])
     for p in peer.values():
         assert topo.may_write(core, p)
         mask &= topo.mask(core, p)
-    ne = len(_bits(mask))
+    eng = _bits(mask)
+    masks = [sum(1 << e for e in eng[::2]), mask, mask]
 
     g.wait_ge(S.ld, 32)
     first = 1
-    spans = []
+    got = []
+    left = 0
     for i, cnt in enumerate(GROUPS):
         dists = range(first, first + cnt)
         ids = []
@@ -50,34 +75,55 @@ def rank_program(g, core, T, topo):
             rid, pid, _ = topo.addr(peer[k])
             ids.append(DstId(rid=rid, pnc=pid))
         g.remote_dma_fused(
-            [RemoteDMATransfer(dst_ids=ids, dma_engine_mask=mask, remote_sem=S["arr%d" % i],
+            [RemoteDMATransfer(dst_ids=ids, dma_engine_mask=masks[i], remote_sem=S["arr%d" % i],
                                srcs=[T.gath[0]], dsts=[T.gath[k] for k in dists], alu_op=0)],
             local_sem=S.sent)
-        spans.append((first if i else 0, first + cnt, S["arr%d" % i], cnt))
+        ne = len(_bits(masks[i]))
+        got.append(ne * cnt)
+        left += ne
         first += cnt
+    mid = 1 + GROUPS[0] + GROUPS[1]
+    assert 1 + GROUPS[0] == T0
 
-    for q, dst, lo, hi in ((g.sync, T.a, 0, HALF), (g.scalar, T.b, HALF, 128)):
+    for q, t0, t1, lo, hi in ((g.sync, T.a0, T.a1, 0, HALF), (g.scalar, T.b0, T.b1, HALF, 128)):
         q.wait_ge(S.ld, 32)
-        for s0, s1, sem, cnt in spans:
-            q.wait_ge(sem, ne * cnt)
-            q.dma_start(dst[8 * s0:8 * s1, :], T.gath[s0:s1, lo:hi, :]).then_inc(S.ab, 16)
+        q.wait_ge(S.arr0, got[0])
+        q.dma_start(t0[0:8 * T0, :], T.gath[0:T0, lo:hi, :]).then_inc(S.ab0, 16)
+        q.wait_ge(S.arr1, got[1])
+        q.dma_start(t1[0:16 * (mid - T0), :], T.gath[T0:mid, lo:hi, :]).then_inc(S.ab1, 16)
+        q.wait_ge(S.arr2, got[2])
+        q.dma_start(t1[16 * (mid - T0):128, :], T.gath[mid:N, lo:hi, :]).then_inc(S.ab1, 16)
 
-    g.tensor.wait_ge(S.ab, 32 * len(spans))
-    g.tensor.matmul(T.pm[:, 0:128], T.a[:, 0:128], T.b[:, 0:128], start=True, stop=False)
-    g.tensor.matmul(T.pm[:, 0:128], T.a[:, 128:256], T.b[:, 128:256], start=False, stop=True).then_inc(S.m1, 1)
-    g.vector.wait_ge(S.m1, 1)
-    g.vector.tensor_copy(T.mt[:], T.pm[:, 0:128]).then_inc(S.c1, 1)
+    k0 = 8 * T0
+    g.tensor.wait_ge(S.ab0, 32)
+    g.tensor.matmul(T.pma[:, 0:64], T.a0[0:k0, 0:128], T.b0[0:k0, 0:64], start=True, stop=False)
+    g.tensor.matmul(T.pma[:, 0:64], T.a0[0:k0, 128:256], T.b0[0:k0, 128:192], start=False, stop=False)
+    g.tensor.matmul(T.pmb[:, 0:64], T.a0[0:k0, 0:128], T.b0[0:k0, 64:128], start=True, stop=False)
+    g.tensor.matmul(T.pmb[:, 0:64], T.a0[0:k0, 128:256], T.b0[0:k0, 192:256], start=False, stop=False)
+    g.tensor.wait_ge(S.ab1, 64)
+    g.tensor.matmul(T.pma[:, 0:64], T.a1[:], T.b1[:, 0:64], start=False, stop=True).then_inc(S.ma, 1)
+    g.tensor.matmul(T.pmb[:, 0:64], T.a1[:], T.b1[:, 64:128], start=False, stop=True).then_inc(S.mb, 1)
+    g.vector.wait_ge(S.ma, 1)
+    g.vector.tensor_copy(T.mt[:, 0:64], T.pma[:, 0:64]).then_inc(S.c1, 1)
+    g.scalar.wait_ge(S.mb, 1)
+    g.scalar.activation(T.mt[:, 64:128], T.pmb[:, 0:64], copy).then_inc(S.c1, 1)
+
     g.tensor.wait_ge(S.xl, 16)
-    g.tensor.wait_ge(S.c1, 1)
-    g.tensor.matmul(T.py0[:, 0:128], T.mt[:], T.xs[:, 0:128], start=True, stop=True).then_inc(S.m20, 1)
-    g.tensor.matmul(T.py1[:, 0:128], T.mt[:], T.xs[:, 128:256], start=True, stop=True).then_inc(S.m21, 1)
-    g.vector.wait_ge(S.m20, 1)
-    g.vector.tensor_copy(T.ys[:, 0:128], T.py0[:, 0:128]).then_inc(S.c20, 1)
-    g.vector.wait_ge(S.m21, 1)
-    g.vector.tensor_copy(T.ys[:, 128:256], T.py1[:, 0:128]).then_inc(S.c21, 1)
-    g.scalar.wait_ge(S.c20, 1)
-    g.scalar.dma_start(T.y[:, 0:128], T.ys[:, 0:128]).then_inc(S.st, 16)
-    g.sync.wait_ge(S.c21, 1)
-    g.sync.dma_start(T.y[:, 128:256], T.ys[:, 128:256]).then_inc(S.st, 16)
+    g.tensor.wait_ge(S.c1, 2)
+    for j in range(4):
+        g.tensor.matmul(T["py%d" % j][:, 0:64], T.mt[:], T.xs[:, 64 * j:64 * j + 64],
+                        start=True, stop=True).then_inc(S["y%d" % j], 1)
+    g.scalar.wait_ge(S.y0, 1)
+    g.scalar.activation(T.ys[:, 0:64], T.py0[:, 0:64], copy).then_inc(S.cy01, 1)
+    g.vector.wait_ge(S.y1, 1)
+    g.vector.tensor_copy(T.ys[:, 64:128], T.py1[:, 0:64]).then_inc(S.cy01, 1)
+    g.scalar.wait_ge(S.y2, 1)
+    g.scalar.activation(T.ys[:, 128:192], T.py2[:, 0:64], copy).then_inc(S.cy23, 1)
+    g.vector.wait_ge(S.y3, 1)
+    g.vector.tensor_copy(T.ys[:, 192:256], T.py3[:, 0:64]).then_inc(S.cy23, 1)
+    g.sync.wait_ge(S.cy01, 2)
+    g.sync.dma_start(T.y[:, 0:128], T.ys[:, 0:128]).then_inc(S.st, 16)
+    g.scalar.wait_ge(S.cy23, 2)
+    g.scalar.dma_start(T.y[:, 128:256], T.ys[:, 128:256]).then_inc(S.st, 16)
     g.sync.wait_ge(S.st, 32)
-    g.wait_ge(S.sent, ne * len(GROUPS))
+    g.wait_ge(S.sent, left)

from concourse.bass import DstId, RemoteDMATransfer
from concourse.mybir import dt, AluOpType, AxisListType, ActivationFunctionType

N = 16
HALF = 64
GROUPS = (7, 6, 2)
T0 = 8

SCRATCH = {
    "gath": ("dram", [N, 128, 32], "bfloat16"),
    "a0": ("sbuf", [128, 256], "bfloat16"),
    "b0": ("sbuf", [128, 256], "bfloat16"),
    "a1": ("sbuf", [128, 128], "bfloat16"),
    "b1": ("sbuf", [128, 128], "bfloat16"),
    "xs": ("sbuf", [128, 256], "bfloat16"),
    "mt": ("sbuf", [128, 128], "bfloat16"),
    "ys": ("sbuf", [128, 256], "bfloat16"),
    "pma": ("psum", [128, 512], "float32"),
    "pmb": ("psum", [128, 512], "float32"),
    "py0": ("psum", [128, 512], "float32"),
    "py1": ("psum", [128, 512], "float32"),
    "py2": ("psum", [128, 512], "float32"),
    "py3": ("psum", [128, 512], "float32"),
}
SEMAPHORES = ["ld", "xl", "arr0", "arr1", "arr2", "sent", "ab0", "ab1", "ma", "mb", "c1",
              "y0", "y1", "y2", "y3", "cy01", "cy23", "st"]


def _bits(mask):
    return [e for e in range(mask.bit_length()) if (mask >> e) & 1]


def _way(topo, a, b):
    ca, cb = topo.chip(a), topo.chip(b)
    if ca == cb:
        return 0
    if topo.mates(ca, cb):
        return 1
    if topo.same_plane(ca, cb):
        return 2
    return 3


def rank_program(g, core, T, topo):
    rank = T.rank_of(core)
    if rank is None:
        return
    S = T.sem
    n = len(T.cores)
    copy = ActivationFunctionType.Copy

    g.sync.dma_start(T.gath[0, 0:HALF, :], T.ut[:]).then_inc(S.ld, 16)
    g.scalar.dma_start(T.gath[0, HALF:128, :], T.vt[:]).then_inc(S.ld, 16)
    g.sync.dma_start(T.xs[:], T.x[:]).then_inc(S.xl, 16)

    assert n & (n - 1) == 0
    order = sorted(range(1, n),
                   key=lambda k: (-max(_way(topo, T.cores[r], T.cores[r ^ k]) for r in range(n)), k))
    peer = {i + 1: T.cores[rank ^ k] for i, k in enumerate(order)}
    mask = topo.mask(core, peer[1])
    for p in peer.values():
        assert topo.may_write(core, p)
        mask &= topo.mask(core, p)
    eng = _bits(mask)
    masks = [sum(1 << e for e in eng[::2]), mask, mask]

    g.wait_ge(S.ld, 32)
    first = 1
    got = []
    left = 0
    for i, cnt in enumerate(GROUPS):
        dists = range(first, first + cnt)
        ids = []
        for k in dists:
            rid, pid, _ = topo.addr(peer[k])
            ids.append(DstId(rid=rid, pnc=pid))
        g.remote_dma_fused(
            [RemoteDMATransfer(dst_ids=ids, dma_engine_mask=masks[i], remote_sem=S["arr%d" % i],
                               srcs=[T.gath[0]], dsts=[T.gath[k] for k in dists], alu_op=0)],
            local_sem=S.sent)
        ne = len(_bits(masks[i]))
        got.append(ne * cnt)
        left += ne
        first += cnt
    mid = 1 + GROUPS[0] + GROUPS[1]
    assert 1 + GROUPS[0] == T0

    for q, t0, t1, lo, hi in ((g.sync, T.a0, T.a1, 0, HALF), (g.scalar, T.b0, T.b1, HALF, 128)):
        q.wait_ge(S.ld, 32)
        q.wait_ge(S.arr0, got[0])
        q.dma_start(t0[0:8 * T0, :], T.gath[0:T0, lo:hi, :]).then_inc(S.ab0, 16)
        q.wait_ge(S.arr1, got[1])
        q.dma_start(t1[0:16 * (mid - T0), :], T.gath[T0:mid, lo:hi, :]).then_inc(S.ab1, 16)
        q.wait_ge(S.arr2, got[2])
        q.dma_start(t1[16 * (mid - T0):128, :], T.gath[mid:N, lo:hi, :]).then_inc(S.ab1, 16)

    k0 = 8 * T0
    g.tensor.wait_ge(S.ab0, 32)
    g.tensor.matmul(T.pma[:, 0:64], T.a0[0:k0, 0:128], T.b0[0:k0, 0:64], start=True, stop=False)
    g.tensor.matmul(T.pma[:, 0:64], T.a0[0:k0, 128:256], T.b0[0:k0, 128:192], start=False, stop=False)
    g.tensor.matmul(T.pmb[:, 0:64], T.a0[0:k0, 0:128], T.b0[0:k0, 64:128], start=True, stop=False)
    g.tensor.matmul(T.pmb[:, 0:64], T.a0[0:k0, 128:256], T.b0[0:k0, 192:256], start=False, stop=False)
    g.tensor.wait_ge(S.ab1, 64)
    g.tensor.matmul(T.pma[:, 0:64], T.a1[:], T.b1[:, 0:64], start=False, stop=True).then_inc(S.ma, 1)
    g.tensor.matmul(T.pmb[:, 0:64], T.a1[:], T.b1[:, 64:128], start=False, stop=True).then_inc(S.mb, 1)
    g.vector.wait_ge(S.ma, 1)
    g.vector.tensor_copy(T.mt[:, 0:64], T.pma[:, 0:64]).then_inc(S.c1, 1)
    g.scalar.wait_ge(S.mb, 1)
    g.scalar.activation(T.mt[:, 64:128], T.pmb[:, 0:64], copy).then_inc(S.c1, 1)

    g.tensor.wait_ge(S.xl, 16)
    g.tensor.wait_ge(S.c1, 2)
    for j in range(4):
        g.tensor.matmul(T["py%d" % j][:, 0:64], T.mt[:], T.xs[:, 64 * j:64 * j + 64],
                        start=True, stop=True).then_inc(S["y%d" % j], 1)
    g.scalar.wait_ge(S.y0, 1)
    g.scalar.activation(T.ys[:, 0:64], T.py0[:, 0:64], copy).then_inc(S.cy01, 1)
    g.vector.wait_ge(S.y1, 1)
    g.vector.tensor_copy(T.ys[:, 64:128], T.py1[:, 0:64]).then_inc(S.cy01, 1)
    g.scalar.wait_ge(S.y2, 1)
    g.scalar.activation(T.ys[:, 128:192], T.py2[:, 0:64], copy).then_inc(S.cy23, 1)
    g.vector.wait_ge(S.y3, 1)
    g.vector.tensor_copy(T.ys[:, 192:256], T.py3[:, 0:64]).then_inc(S.cy23, 1)
    g.sync.wait_ge(S.cy01, 2)
    g.sync.dma_start(T.y[:, 0:128], T.ys[:, 0:128]).then_inc(S.st, 16)
    g.scalar.wait_ge(S.cy23, 2)
    g.scalar.dma_start(T.y[:, 128:256], T.ys[:, 128:256]).then_inc(S.st, 16)
    g.sync.wait_ge(S.st, 32)
    g.wait_ge(S.sent, left)
